import numpy as np
import ml_dtypes


def mxq(x, axis, fmt="e4m3"):
    dtype, down = {"e4m3": (ml_dtypes.float8_e4m3fn, 7), "e5m2": (ml_dtypes.float8_e5m2, 14)}[fmt]
    v = np.moveaxis(np.asarray(x, np.float32).astype(ml_dtypes.bfloat16).astype(np.float64), axis, -1)
    blocks = v.reshape(v.shape[:-1] + (-1, 32))
    amax = np.abs(blocks).max(-1, keepdims=True)
    byte = np.maximum(np.where(amax > 0, np.frexp(amax)[1] - 1 + 127, 0) - down, 1)
    scale = np.exp2(byte - 127.0)
    codes = (blocks / scale).astype(np.float32).astype(dtype).astype(np.float64)
    return np.moveaxis((codes * scale).reshape(v.shape), -1, axis)


WIDE = False


def mx_kscale(k):
    if not WIDE:
        return np.ones(k)
    levels = np.array([10, -10, 5, -5, 0])
    if k % 512:
        return np.exp2(np.random.permutation(np.resize(levels, k // 32))).repeat(32)
    a = np.empty((k // 512, 16))
    for p in range(k // 512):
        a[p, :8] = np.random.permutation(np.resize(levels, 8))
        for g in range(8):
            far = levels[np.abs(levels - a[p, g]) >= 10]
            a[p, g + 8] = far[np.random.randint(len(far))]
    return np.exp2(a.ravel()).repeat(32)


def f64(x):
    return np.asarray(x).astype(np.float64)


def striped(idx):
    return np.tile(idx.reshape(-1, 16).T, (8, 1)).astype(np.uint16)


def unstriped(offs):
    return offs[:16].T.reshape(-1).astype(np.int64)


E2M1 = np.array([0.0, 0.5, 1.0, 1.5, 2.0, 3.0, 4.0, 6.0, -0.0, -0.5, -1.0, -1.5, -2.0, -3.0, -4.0, -6.0])


def pack_weight(w, fmt):
    k, n = w.shape
    w = f64(np.asarray(w, np.float32).astype(ml_dtypes.bfloat16)).reshape(k // 32, 32, n)
    amax = np.abs(w).max(1)
    if fmt == "e4m3":
        byte = np.frexp(amax)[1] - 1 + 127 - 7
    else:
        mant, ex = np.frexp(amax / 6.0)
        byte = np.where(mant > 0.5, ex, ex - 1) + 127
    byte = np.clip(np.where(amax > 0, byte, 1), 1, 254)
    scaled = (w * np.exp2(127.0 - byte)[:, None, :]).reshape(k, n).astype(np.float32)
    by_word = np.ascontiguousarray(scaled.reshape(k // 512, 128, 4, n).transpose(0, 1, 3, 2))
    if fmt == "e4m3":
        words = by_word.astype(ml_dtypes.float8_e4m3fn).view(np.uint8)
    else:
        c = by_word.astype(ml_dtypes.float4_e2m1fn).view(np.uint8) & 0xF
        words = (c[..., 0::2] | (c[..., 1::2] << 4)).reshape(k // 512, 128, 2 * n)
    return np.ascontiguousarray(words), np.ascontiguousarray(byte.astype(np.uint8).reshape(k // 512, 16, n))


def unpack_weight(words, scales, fmt):
    g, _, n = scales.shape
    words = np.ascontiguousarray(words).reshape(g, 128, n, -1)
    if fmt == "e4m3":
        vals = words.view(ml_dtypes.float8_e4m3fn).astype(np.float64)
    else:
        nib = np.empty((g, 128, n, 4), np.uint8)
        nib[..., 0::2] = words & 0xF
        nib[..., 1::2] = words >> 4
        vals = E2M1[nib]
    vals = vals * np.repeat(np.exp2(scales.astype(np.float64) - 127.0), 8, axis=1)[..., None]
    return vals.transpose(0, 1, 3, 2).reshape(g * 512, n)


def pack_table4(v):
    words, scales = pack_weight(v, "e2m1")
    g, t = words.shape[0] // 2, v.shape[1]
    words = words.reshape(g, 2, 128, t, 2).transpose(0, 2, 3, 1, 4)
    return np.concatenate([words.reshape(g, -1), scales.reshape(g, -1)], axis=1)


def unpack_table4(tab):
    g, t = tab.shape[0], tab.shape[1] // 544
    words = tab[:, :512 * t].reshape(g, 128, t, 2, 2).transpose(0, 3, 1, 2, 4).reshape(2 * g, 128, 2 * t)
    return unpack_weight(words, tab[:, 512 * t:].reshape(2 * g, 16, t), "e2m1")


def pack_table(v):
    words, scales = pack_weight(v, "e4m3")
    return np.concatenate([words.reshape(words.shape[0], -1), scales.reshape(scales.shape[0], -1)], axis=1)


def unpack_table(tab):
    g, t = tab.shape[0], tab.shape[1] // 528
    return unpack_weight(tab[:, :512 * t].reshape(g, 128, t, 4), tab[:, 512 * t:].reshape(g, 16, t), "e4m3")


K, L, M, T, S = 512, 1024, 256, 4096, 2048


def setup_inputs():
    n = np.random.standard_normal
    s1 = mx_kscale(K)[:, None]
    s2 = mx_kscale(L)[:, None]
    p_w4 = pack_weight(n((K, M)) / np.sqrt(K) / s1, "e2m1")
    return {
        "tab": pack_table(n((K, T)) * s1),
        "w4_words": p_w4[0],
        "w4_scales": p_w4[1],
        "tab2": pack_table4(n((L, T)) * s2),
        "u": (n((L, M)) / np.sqrt(L) / s2).astype(np.float32),
        "offs": striped(np.random.permutation(T)[:S]),
        "offs2": striped(np.random.permutation(T)[:S]),
    }


def reference(tab, w4_words, w4_scales, tab2, u, offs, offs2):
    tab_ = unpack_table(tab)[:, unstriped(offs)]
    w4_ = unpack_weight(w4_words, w4_scales, "e2m1")
    tab2_ = unpack_table4(tab2)[:, unstriped(offs2)]
    u_ = mxq(f64(u), 0, "e4m3")
    y = tab_.T @ w4_ + tab2_.T @ u_
    return y

@@ -1,0 +1,155 @@
+from contextlib import ExitStack
+
+import concourse.mybir as mybir
+
+K, L, M, T, S = 512, 1024, 256, 4096, 2048
+FLOPS = 2 * S * M * (K + L)
+
+F32 = mybir.dt.float32
+BF16 = mybir.dt.bfloat16
+I32 = mybir.dt.int32
+U32 = mybir.dt.uint32
+U16 = mybir.dt.uint16
+U8 = mybir.dt.uint8
+E4M3 = mybir.dt.float8_e4m3fn_x4
+E2M1 = mybir.dt.float4_e2m1fn_x4
+
+P = 128
+SLICE = 512
+HALF = 128
+ROW = T
+H0_ROW = 12
+H1_ROW = 28
+
+
+def tile_list_tab48_tm_none_kernel(tc, tab, w4_words, w4_scales, tab2, u, offs, offs2, out):
+    nc = tc.nc
+    with ExitStack() as ctx:
+        keep = ctx.enter_context(tc.tile_pool(name="keep", bufs=1))
+        ring = ctx.enter_context(tc.tile_pool(name="ring", bufs=4))
+        psum = ctx.enter_context(tc.psum_pool(name="psum", bufs=1))
+
+        idx1 = keep.tile([P, S // 16], U16, name="idx1")
+        idx2 = keep.tile([P, S // 16], U16, name="idx2")
+        tab_words = keep.tile([P, T], I32, name="tab_words", align_bytes=64)
+        tab2_words = keep.tile([P, T], I32, name="tab2_words", align_bytes=64)
+        tab_scales = keep.tile([P, T], U8, name="tab_scales", align_bytes=64)
+        tab2_scales = keep.tile([P, T], U8, name="tab2_scales", align_bytes=64)
+        w4_codes = keep.tile([P, 2 * M], U8, name="w4_codes", align_bytes=64)
+        w4_plane = keep.tile([P, M], U8, name="w4_plane", align_bytes=64)
+        u_raw = keep.tile([P, 2, 4, M], F32, name="u_raw", align_bytes=64)
+        u_grouped = keep.tile([P, 2, M, 4], BF16, name="u_grouped", align_bytes=64)
+        u_codes = keep.tile([P, 2 * M], U32, name="u_codes", align_bytes=64)
+        u_plane = keep.tile([P, 2 * M], U8, name="u_plane", align_bytes=64)
+        picked_scales2 = keep.tile([P, S], U8, name="picked_scales2", align_bytes=64)
+        plane1 = keep.tile([P, S], U8, name="plane1", align_bytes=64)
+        plane2 = keep.tile([P, 2, S], U8, name="plane2", align_bytes=64)
+
+        nc.vector.memset(tab_scales[:].bitcast(I32), 0)
+        nc.gpsimd.memset(w4_plane[:].bitcast(I32), 0)
+        nc.gpsimd.memset(plane2[:].rearrange("p h j -> p (h j)").bitcast(I32), 0)
+
+        nc.sync.dma_start(idx2[:], offs2)
+        words2 = T * 4 * P
+        for q in range(4):
+            first = words2 + (4 * q - H0_ROW) * ROW
+            nc.sync.dma_start(
+                tab2_scales[32 * q : 32 * q + 32, :].bitcast(I32),
+                tab2[0, first : first + 32 * ROW].rearrange("(p t) -> p t", t=ROW).bitcast(I32),
+            )
+        for q in range(4):
+            first = words2 + 4 * q * ROW
+            nc.scalar.dma_start(
+                tab_scales[32 * q : 32 * q + 4, :].bitcast(I32),
+                tab[0, first : first + 4 * ROW].rearrange("(p t) -> p t", t=ROW).bitcast(I32),
+            )
+        nc.sync.dma_start(idx1[:], offs)
+
+        def load_words(tile, table):
+            rows = table[0, 0:words2].rearrange("(p b) -> p b", p=P).bitcast(I32)
+            for c in range(2):
+                cols = slice(c * T // 2, (c + 1) * T // 2)
+                nc.sync.dma_start(tile[:, cols], rows[:, cols])
+
+        load_words(tab_words, tab)
+        nc.sync.dma_start(u_raw[:], u.rearrange("(a p j) n -> p a j n", p=P, j=4))
+        load_words(tab2_words, tab2)
+        nc.gpsimd.dma_start(w4_codes[:].bitcast(I32), w4_words[0].bitcast(I32))
+        for q in range(4):
+            nc.gpsimd.dma_start(w4_plane[32 * q : 32 * q + 4, :].bitcast(I32), w4_scales[0, 4 * q : 4 * q + 4, :].bitcast(I32))
+
+        nc.vector.tensor_copy(picked_scales2[:], tab2_scales[:].indirect(idx2[:]))
+        for h, row in ((0, H0_ROW), (1, H1_ROW)):
+            for q in range(4):
+                nc.sync.dma_start(
+                    plane2[32 * q : 32 * q + 4, h, :].bitcast(I32),
+                    picked_scales2[32 * q + row : 32 * q + row + 4, :].bitcast(I32),
+                )
+        nc.vector.tensor_copy(plane1[:], tab_scales[:].indirect(idx1[:]))
+
+        for a in range(2):
+            nc.scalar.copy(u_grouped[:, a], u_raw[:, a].rearrange("p j n -> p n j"))
+
+        def gather(tile, idx, s, name):
+            picked = ring.tile([P, SLICE], I32, name=name, align_bytes=64)
+            nc.vector.tensor_copy(
+                picked[:].bitcast(U32),
+                tile[:].bitcast(U32).indirect(idx[:, s * SLICE // 16 : (s + 1) * SLICE // 16]),
+            )
+            return picked
+
+        slices = S // SLICE
+        for s in range(slices):
+            last = s == slices - 1
+            words1 = gather(tab_words, idx1, s, "words1")
+            if s == 0:
+                nc.vector.quantize_mx(
+                    out=u_codes[:].bitcast(E4M3),
+                    scales=u_plane[:],
+                    in_=u_grouped[:].rearrange("p a n j -> p (a n j)"),
+                )
+            pairs = gather(tab2_words, idx2, s, "pairs")
+            codes2 = ring.tile([P, 2, 2 * SLICE], U8, name="codes2", align_bytes=64)
+            nc.vector.tensor_copy(
+                codes2[:].bitcast(U16),
+                pairs[:].bitcast(U16).rearrange("p (j h) -> p h j", h=2),
+            )
+            sums = {}
+            for i in range(SLICE // P):
+                for half in range(2):
+                    bank = psum.tile([P, HALF], F32, name=f"bank{2 * i + half}")
+                    sums[i, half] = bank
+                    n0 = half * HALF
+                    nc.tensor.matmul_mx(
+                        out=bank[:],
+                        lhsT=words1[:, i * P : (i + 1) * P].bitcast(E4M3),
+                        lhsT_scale=plane1[:, s * SLICE + i * P : s * SLICE + (i + 1) * P],
+                        rhs=w4_codes[:, 2 * n0 : 2 * (n0 + HALF)].bitcast(E2M1),
+                        rhs_scale=w4_plane[:, n0 : n0 + HALF],
+                        start=True,
+                        stop=False,
+                    )
+            staged = ring.tile([P, SLICE // P, M], F32, name="staged")
+            rows = out[s * SLICE : (s + 1) * SLICE, :].rearrange("(i p) n -> p i n", p=P)
+            for i in range(SLICE // P):
+                for half in range(2):
+                    n0 = half * HALF
+                    bank = sums[i, half]
+                    for h in range(2):
+                        nc.tensor.matmul_mx(
+                            out=bank[:],
+                            lhsT=codes2[:, h, 2 * i * P : 2 * (i + 1) * P].bitcast(E2M1),
+                            lhsT_scale=plane2[:, h, s * SLICE + i * P : s * SLICE + (i + 1) * P],
+                            rhs=u_codes[:, h * M + n0 : h * M + n0 + HALF].bitcast(E4M3),
+                            rhs_scale=u_plane[:, h * M + n0 : h * M + n0 + HALF],
+                            start=False,
+                            stop=h == 1,
+                        )
+                    if last and half == 1:
+                        nc.vector.tensor_copy(staged[:, i, n0 : n0 + HALF], bank[:])
+                    else:
+                        nc.scalar.copy(staged[:, i, n0 : n0 + HALF], bank[:])
+                if last:
+                    nc.sync.dma_start(rows[:, i], staged[:, i])
+            if not last:
+                nc.sync.dma_start(rows, staged[:])

@@ -17,16 +17,14 @@ E2M1 = mybir.dt.float4_e2m1fn_x4
 P = 128
 SLICE = 512
 HALF = 128
-ROW = T
-H0_ROW = 12
-H1_ROW = 28
+WORD_BYTES = P * T * 4
 
 
 def tile_list_tab48_tm_none_kernel(tc, tab, w4_words, w4_scales, tab2, u, offs, offs2, out):
     nc = tc.nc
     with ExitStack() as ctx:
         keep = ctx.enter_context(tc.tile_pool(name="keep", bufs=1))
-        ring = ctx.enter_context(tc.tile_pool(name="ring", bufs=4))
+        ring = ctx.enter_context(tc.tile_pool(name="ring", bufs=2))
         psum = ctx.enter_context(tc.psum_pool(name="psum", bufs=1))
 
         idx1 = keep.tile([P, S // 16], U16, name="idx1")
@@ -42,114 +40,132 @@ def tile_list_tab48_tm_none_kernel(tc, tab, w4_words, w4_scales, tab2, u, offs, 
         u_codes = keep.tile([P, 2 * M], U32, name="u_codes", align_bytes=64)
         u_plane = keep.tile([P, 2 * M], U8, name="u_plane", align_bytes=64)
         picked_scales2 = keep.tile([P, S], U8, name="picked_scales2", align_bytes=64)
+        picked_scales1 = keep.tile([P, S], U8, name="picked_scales1", align_bytes=64)
         plane1 = keep.tile([P, S], U8, name="plane1", align_bytes=64)
         plane2 = keep.tile([P, 2, S], U8, name="plane2", align_bytes=64)
 
-        nc.vector.memset(tab_scales[:].bitcast(I32), 0)
-        nc.gpsimd.memset(w4_plane[:].bitcast(I32), 0)
-        nc.gpsimd.memset(plane2[:].rearrange("p h j -> p (h j)").bitcast(I32), 0)
-
         nc.sync.dma_start(idx2[:], offs2)
-        words2 = T * 4 * P
-        for q in range(4):
-            first = words2 + (4 * q - H0_ROW) * ROW
-            nc.sync.dma_start(
-                tab2_scales[32 * q : 32 * q + 32, :].bitcast(I32),
-                tab2[0, first : first + 32 * ROW].rearrange("(p t) -> p t", t=ROW).bitcast(I32),
-            )
-        for q in range(4):
-            first = words2 + 4 * q * ROW
-            nc.scalar.dma_start(
-                tab_scales[32 * q : 32 * q + 4, :].bitcast(I32),
-                tab[0, first : first + 4 * ROW].rearrange("(p t) -> p t", t=ROW).bitcast(I32),
-            )
+        nc.sync.dma_start(
+            tab2_scales[0:32, :].bitcast(I32),
+            tab2[0, WORD_BYTES : WORD_BYTES + 32 * T].rearrange("(p t) -> p t", t=T).bitcast(I32),
+        )
         nc.sync.dma_start(idx1[:], offs)
+        nc.sync.dma_start(
+            tab_scales[0:32, :].bitcast(I32),
+            tab[0, WORD_BYTES - 16 * T : WORD_BYTES + 16 * T].rearrange("(p t) -> p t", t=T).bitcast(I32),
+        )
+        nc.gpsimd.memset(tab2_scales[64:128, :].bitcast(I32), 0)
+        nc.vector.memset(tab2_scales[32:64, :].bitcast(I32), 0)
+        nc.vector.memset(tab_scales[32:64, :].bitcast(I32), 0)
+        nc.gpsimd.memset(tab_scales[64:128, :].bitcast(I32), 0)
+        nc.gpsimd.memset(w4_plane[:].bitcast(I32), 0)
 
-        def load_words(tile, table):
-            rows = table[0, 0:words2].rearrange("(p b) -> p b", p=P).bitcast(I32)
-            for c in range(2):
-                cols = slice(c * T // 2, (c + 1) * T // 2)
-                nc.sync.dma_start(tile[:, cols], rows[:, cols])
-
-        load_words(tab_words, tab)
         nc.sync.dma_start(u_raw[:], u.rearrange("(a p j) n -> p a j n", p=P, j=4))
-        load_words(tab2_words, tab2)
+        for tile, table in ((tab2_words, tab2), (tab_words, tab)):
+            nc.sync.dma_start(tile[:], table[0, 0:WORD_BYTES].rearrange("(p b) -> p b", p=P).bitcast(I32))
         nc.gpsimd.dma_start(w4_codes[:].bitcast(I32), w4_words[0].bitcast(I32))
         for q in range(4):
             nc.gpsimd.dma_start(w4_plane[32 * q : 32 * q + 4, :].bitcast(I32), w4_scales[0, 4 * q : 4 * q + 4, :].bitcast(I32))
 
-        nc.vector.tensor_copy(picked_scales2[:], tab2_scales[:].indirect(idx2[:]))
-        for h, row in ((0, H0_ROW), (1, H1_ROW)):
-            for q in range(4):
-                nc.sync.dma_start(
-                    plane2[32 * q : 32 * q + 4, h, :].bitcast(I32),
-                    picked_scales2[32 * q + row : 32 * q + row + 4, :].bitcast(I32),
-                )
-        nc.vector.tensor_copy(plane1[:], tab_scales[:].indirect(idx1[:]))
-
         for a in range(2):
             nc.scalar.copy(u_grouped[:, a], u_raw[:, a].rearrange("p j n -> p n j"))
 
-        def gather(tile, idx, s, name):
+        def shift(plane, picked, first):
+            for q in range(4):
+                nc.sync.dma_start(
+                    plane[32 * q : 32 * q + 32, :].bitcast(I32),
+                    picked[first + 4 * q : first + 4 * q + 32, :].bitcast(I32),
+                )
+
+        nc.vector.tensor_copy(picked_scales2[:], tab2_scales[:].indirect(idx2[:]))
+        for h in range(2):
+            shift(plane2[:, h, :], picked_scales2, 16 * h)
+        nc.vector.quantize_mx(
+            out=u_codes[:].bitcast(E4M3),
+            scales=u_plane[:],
+            in_=u_grouped[:].rearrange("p a n j -> p (a n j)"),
+        )
+        nc.vector.tensor_copy(picked_scales1[:], tab_scales[:].indirect(idx1[:]))
+        shift(plane1, picked_scales1, 16)
+
+        slices = S // SLICE
+        tiles = SLICE // P
+        pairs, words1, codes2, sums = {}, {}, {}, {}
+
+        def gather_words(kept, tile, idx, s, name):
             picked = ring.tile([P, SLICE], I32, name=name, align_bytes=64)
             nc.vector.tensor_copy(
                 picked[:].bitcast(U32),
                 tile[:].bitcast(U32).indirect(idx[:, s * SLICE // 16 : (s + 1) * SLICE // 16]),
             )
-            return picked
+            kept[s] = picked
 
-        slices = S // SLICE
-        for s in range(slices):
-            last = s == slices - 1
-            words1 = gather(tab_words, idx1, s, "words1")
-            if s == 0:
-                nc.vector.quantize_mx(
-                    out=u_codes[:].bitcast(E4M3),
-                    scales=u_plane[:],
-                    in_=u_grouped[:].rearrange("p a n j -> p (a n j)"),
+        def part(s):
+            codes2[s] = ring.tile([P, 2, 2 * SLICE], U8, name="codes2", align_bytes=64)
+            nc.vector.tensor_copy(codes2[s][:].bitcast(U16), pairs[s][:].bitcast(U16).rearrange("p (j h) -> p h j", h=2))
+
+        def open_group(s, i, half):
+            n0 = half * HALF
+            for h in range(2):
+                nc.tensor.matmul_mx(
+                    out=sums[s, i, half],
+                    lhsT=codes2[s][:, h, 2 * i * P : 2 * (i + 1) * P].bitcast(E2M1),
+                    lhsT_scale=plane2[:, h, s * SLICE + i * P : s * SLICE + (i + 1) * P],
+                    rhs=u_codes[:, h * M + n0 : h * M + n0 + HALF].bitcast(E4M3),
+                    rhs_scale=u_plane[:, h * M + n0 : h * M + n0 + HALF],
+                    start=h == 0,
+                    stop=False,
                 )
-            pairs = gather(tab2_words, idx2, s, "pairs")
-            codes2 = ring.tile([P, 2, 2 * SLICE], U8, name="codes2", align_bytes=64)
-            nc.vector.tensor_copy(
-                codes2[:].bitcast(U16),
-                pairs[:].bitcast(U16).rearrange("p (j h) -> p h j", h=2),
+
+        def close_group(s, i, half):
+            n0 = half * HALF
+            nc.tensor.matmul_mx(
+                out=sums[s, i, half],
+                lhsT=words1[s][:, i * P : (i + 1) * P].bitcast(E4M3),
+                lhsT_scale=plane1[:, s * SLICE + i * P : s * SLICE + (i + 1) * P],
+                rhs=w4_codes[:, 2 * n0 : 2 * (n0 + HALF)].bitcast(E2M1),
+                rhs_scale=w4_plane[:, n0 : n0 + HALF],
+                start=False,
+                stop=True,
             )
-            sums = {}
-            for i in range(SLICE // P):
+
+        def open_slice(s):
+            for i in range(tiles):
+                bank = psum.tile([P, 2, HALF], F32, name=f"bank{s % 2 * 4 + i}")
                 for half in range(2):
-                    bank = psum.tile([P, HALF], F32, name=f"bank{2 * i + half}")
-                    sums[i, half] = bank
-                    n0 = half * HALF
-                    nc.tensor.matmul_mx(
-                        out=bank[:],
-                        lhsT=words1[:, i * P : (i + 1) * P].bitcast(E4M3),
-                        lhsT_scale=plane1[:, s * SLICE + i * P : s * SLICE + (i + 1) * P],
-                        rhs=w4_codes[:, 2 * n0 : 2 * (n0 + HALF)].bitcast(E2M1),
-                        rhs_scale=w4_plane[:, n0 : n0 + HALF],
-                        start=True,
-                        stop=False,
-                    )
-            staged = ring.tile([P, SLICE // P, M], F32, name="staged")
+                    sums[s, i, half] = bank[:, half]
+                if s == slices - 1:
+                    other = psum.tile([P, 2, HALF], F32, name=f"bank{(s + 1) % 2 * 4 + i}")
+                    sums[s, i, 1] = other[:, 1]
+                sums[s, i] = bank
+            for i in range(tiles):
+                open_group(s, i, 0)
+                if s == slices - 1:
+                    open_group(s, i, 1)
+
+        def close_slice(s):
+            staged = keep.tile([P, tiles, M], F32, name=f"staged{s}")
             rows = out[s * SLICE : (s + 1) * SLICE, :].rearrange("(i p) n -> p i n", p=P)
-            for i in range(SLICE // P):
-                for half in range(2):
-                    n0 = half * HALF
-                    bank = sums[i, half]
-                    for h in range(2):
-                        nc.tensor.matmul_mx(
-                            out=bank[:],
-                            lhsT=codes2[:, h, 2 * i * P : 2 * (i + 1) * P].bitcast(E2M1),
-                            lhsT_scale=plane2[:, h, s * SLICE + i * P : s * SLICE + (i + 1) * P],
-                            rhs=u_codes[:, h * M + n0 : h * M + n0 + HALF].bitcast(E4M3),
-                            rhs_scale=u_plane[:, h * M + n0 : h * M + n0 + HALF],
-                            start=False,
-                            stop=h == 1,
-                        )
-                    if last and half == 1:
-                        nc.vector.tensor_copy(staged[:, i, n0 : n0 + HALF], bank[:])
-                    else:
-                        nc.scalar.copy(staged[:, i, n0 : n0 + HALF], bank[:])
-                if last:
+            for i in range(tiles):
+                if s < slices - 1:
+                    close_group(s, i, 0)
+                    open_group(s, i, 1)
+                    close_group(s, i, 1)
+                    nc.scalar.copy(staged[:, i], sums[s, i][:].rearrange("p h n -> p (h n)"))
+                else:
+                    for half in range(2):
+                        close_group(s, i, half)
+                    nc.scalar.copy(staged[:, i, 0:HALF], sums[s, i, 0])
+                    nc.vector.tensor_copy(staged[:, i, HALF:M], sums[s, i, 1])
                     nc.sync.dma_start(rows[:, i], staged[:, i])
-            if not last:
+            if s < slices - 1:
                 nc.sync.dma_start(rows, staged[:])
+
+        gather_words(pairs, tab2_words, idx2, 0, "pairs")
+        for s in range(slices):
+            if s + 1 < slices:
+                gather_words(pairs, tab2_words, idx2, s + 1, "pairs")
+            part(s)
+            open_slice(s)
+            gather_words(words1, tab_words, idx1, s, "words1")
+            close_slice(s)

@@ -49,44 +49,42 @@ def tile_list_tab48_tm_none_kernel(tc, tab, w4_words, w4_scales, tab2, u, offs, 
             tab2_scales[0:32, :].bitcast(I32),
             tab2[0, WORD_BYTES : WORD_BYTES + 32 * T].rearrange("(p t) -> p t", t=T).bitcast(I32),
         )
+        nc.vector.memset(tab2_scales[32:64, :].bitcast(I32), 0)
+        nc.vector.memset(tab2_scales[64:128, :].bitcast(I32), 0)
+        nc.gpsimd.memset(w4_plane[:].bitcast(I32), 0)
+        nc.gpsimd.memset(plane1[:].bitcast(I32), 0)
         nc.sync.dma_start(idx1[:], offs)
         nc.sync.dma_start(
-            tab_scales[0:32, :].bitcast(I32),
-            tab[0, WORD_BYTES - 16 * T : WORD_BYTES + 16 * T].rearrange("(p t) -> p t", t=T).bitcast(I32),
+            tab_scales[:].bitcast(I32),
+            tab[0, WORD_BYTES - 112 * T : WORD_BYTES + 16 * T].rearrange("(p t) -> p t", t=T).bitcast(I32),
         )
-        nc.gpsimd.memset(tab2_scales[64:128, :].bitcast(I32), 0)
-        nc.vector.memset(tab2_scales[32:64, :].bitcast(I32), 0)
-        nc.vector.memset(tab_scales[32:64, :].bitcast(I32), 0)
-        nc.gpsimd.memset(tab_scales[64:128, :].bitcast(I32), 0)
-        nc.gpsimd.memset(w4_plane[:].bitcast(I32), 0)
-
         nc.sync.dma_start(u_raw[:], u.rearrange("(a p j) n -> p a j n", p=P, j=4))
+        nc.scalar.dma_start(w4_codes[:].bitcast(I32), w4_words[0].bitcast(I32))
+        for q in range(4):
+            nc.scalar.dma_start(w4_plane[32 * q : 32 * q + 4, :].bitcast(I32), w4_scales[0, 4 * q : 4 * q + 4, :].bitcast(I32))
         for tile, table in ((tab2_words, tab2), (tab_words, tab)):
             nc.sync.dma_start(tile[:], table[0, 0:WORD_BYTES].rearrange("(p b) -> p b", p=P).bitcast(I32))
-        nc.gpsimd.dma_start(w4_codes[:].bitcast(I32), w4_words[0].bitcast(I32))
-        for q in range(4):
-            nc.gpsimd.dma_start(w4_plane[32 * q : 32 * q + 4, :].bitcast(I32), w4_scales[0, 4 * q : 4 * q + 4, :].bitcast(I32))
 
         for a in range(2):
             nc.scalar.copy(u_grouped[:, a], u_raw[:, a].rearrange("p j n -> p n j"))
 
-        def shift(plane, picked, first):
+        def shift(queue, plane, picked, first, rows):
             for q in range(4):
-                nc.sync.dma_start(
-                    plane[32 * q : 32 * q + 32, :].bitcast(I32),
-                    picked[first + 4 * q : first + 4 * q + 32, :].bitcast(I32),
+                queue.dma_start(
+                    plane[32 * q : 32 * q + rows, :].bitcast(I32),
+                    picked[first + 4 * q : first + 4 * q + rows, :].bitcast(I32),
                 )
 
         nc.vector.tensor_copy(picked_scales2[:], tab2_scales[:].indirect(idx2[:]))
         for h in range(2):
-            shift(plane2[:, h, :], picked_scales2, 16 * h)
+            shift(nc.scalar, plane2[:, h, :], picked_scales2, 16 * h, 32)
         nc.vector.quantize_mx(
             out=u_codes[:].bitcast(E4M3),
             scales=u_plane[:],
             in_=u_grouped[:].rearrange("p a n j -> p (a n j)"),
         )
         nc.vector.tensor_copy(picked_scales1[:], tab_scales[:].indirect(idx1[:]))
-        shift(plane1, picked_scales1, 16)
+        shift(nc.sync, plane1, picked_scales1, 112, 4)
 
         slices = S // SLICE
         tiles = SLICE // P

from contextlib import ExitStack

import concourse.mybir as mybir

K, L, M, T, S = 512, 1024, 256, 4096, 2048
FLOPS = 2 * S * M * (K + L)

F32 = mybir.dt.float32
BF16 = mybir.dt.bfloat16
I32 = mybir.dt.int32
U32 = mybir.dt.uint32
U16 = mybir.dt.uint16
U8 = mybir.dt.uint8
E4M3 = mybir.dt.float8_e4m3fn_x4
E2M1 = mybir.dt.float4_e2m1fn_x4

P = 128
SLICE = 512
HALF = 128
WORD_BYTES = P * T * 4


def tile_list_tab48_tm_none_kernel(tc, tab, w4_words, w4_scales, tab2, u, offs, offs2, out):
    nc = tc.nc
    with ExitStack() as ctx:
        keep = ctx.enter_context(tc.tile_pool(name="keep", bufs=1))
        ring = ctx.enter_context(tc.tile_pool(name="ring", bufs=2))
        psum = ctx.enter_context(tc.psum_pool(name="psum", bufs=1))

        idx1 = keep.tile([P, S // 16], U16, name="idx1")
        idx2 = keep.tile([P, S // 16], U16, name="idx2")
        tab_words = keep.tile([P, T], I32, name="tab_words", align_bytes=64)
        tab2_words = keep.tile([P, T], I32, name="tab2_words", align_bytes=64)
        tab_scales = keep.tile([P, T], U8, name="tab_scales", align_bytes=64)
        tab2_scales = keep.tile([P, T], U8, name="tab2_scales", align_bytes=64)
        w4_codes = keep.tile([P, 2 * M], U8, name="w4_codes", align_bytes=64)
        w4_plane = keep.tile([P, M], U8, name="w4_plane", align_bytes=64)
        u_raw = keep.tile([P, 2, 4, M], F32, name="u_raw", align_bytes=64)
        u_grouped = keep.tile([P, 2, M, 4], BF16, name="u_grouped", align_bytes=64)
        u_codes = keep.tile([P, 2 * M], U32, name="u_codes", align_bytes=64)
        u_plane = keep.tile([P, 2 * M], U8, name="u_plane", align_bytes=64)
        picked_scales2 = keep.tile([P, S], U8, name="picked_scales2", align_bytes=64)
        picked_scales1 = keep.tile([P, S], U8, name="picked_scales1", align_bytes=64)
        plane1 = keep.tile([P, S], U8, name="plane1", align_bytes=64)
        plane2 = keep.tile([P, 2, S], U8, name="plane2", align_bytes=64)

        nc.sync.dma_start(idx2[:], offs2)
        nc.sync.dma_start(
            tab2_scales[0:32, :].bitcast(I32),
            tab2[0, WORD_BYTES : WORD_BYTES + 32 * T].rearrange("(p t) -> p t", t=T).bitcast(I32),
        )
        nc.vector.memset(tab2_scales[32:64, :].bitcast(I32), 0)
        nc.vector.memset(tab2_scales[64:128, :].bitcast(I32), 0)
        nc.gpsimd.memset(w4_plane[:].bitcast(I32), 0)
        nc.gpsimd.memset(plane1[:].bitcast(I32), 0)
        nc.sync.dma_start(idx1[:], offs)
        nc.sync.dma_start(
            tab_scales[:].bitcast(I32),
            tab[0, WORD_BYTES - 112 * T : WORD_BYTES + 16 * T].rearrange("(p t) -> p t", t=T).bitcast(I32),
        )
        nc.sync.dma_start(u_raw[:], u.rearrange("(a p j) n -> p a j n", p=P, j=4))
        nc.scalar.dma_start(w4_codes[:].bitcast(I32), w4_words[0].bitcast(I32))
        for q in range(4):
            nc.scalar.dma_start(w4_plane[32 * q : 32 * q + 4, :].bitcast(I32), w4_scales[0, 4 * q : 4 * q + 4, :].bitcast(I32))
        for tile, table in ((tab2_words, tab2), (tab_words, tab)):
            nc.sync.dma_start(tile[:], table[0, 0:WORD_BYTES].rearrange("(p b) -> p b", p=P).bitcast(I32))

        for a in range(2):
            nc.scalar.copy(u_grouped[:, a], u_raw[:, a].rearrange("p j n -> p n j"))

        def shift(queue, plane, picked, first, rows):
            for q in range(4):
                queue.dma_start(
                    plane[32 * q : 32 * q + rows, :].bitcast(I32),
                    picked[first + 4 * q : first + 4 * q + rows, :].bitcast(I32),
                )

        nc.vector.tensor_copy(picked_scales2[:], tab2_scales[:].indirect(idx2[:]))
        for h in range(2):
            shift(nc.scalar, plane2[:, h, :], picked_scales2, 16 * h, 32)
        nc.vector.quantize_mx(
            out=u_codes[:].bitcast(E4M3),
            scales=u_plane[:],
            in_=u_grouped[:].rearrange("p a n j -> p (a n j)"),
        )
        nc.vector.tensor_copy(picked_scales1[:], tab_scales[:].indirect(idx1[:]))
        shift(nc.sync, plane1, picked_scales1, 112, 4)

        slices = S // SLICE
        tiles = SLICE // P
        pairs, words1, codes2, sums = {}, {}, {}, {}

        def gather_words(kept, tile, idx, s, name):
            picked = ring.tile([P, SLICE], I32, name=name, align_bytes=64)
            nc.vector.tensor_copy(
                picked[:].bitcast(U32),
                tile[:].bitcast(U32).indirect(idx[:, s * SLICE // 16 : (s + 1) * SLICE // 16]),
            )
            kept[s] = picked

        def part(s):
            codes2[s] = ring.tile([P, 2, 2 * SLICE], U8, name="codes2", align_bytes=64)
            nc.vector.tensor_copy(codes2[s][:].bitcast(U16), pairs[s][:].bitcast(U16).rearrange("p (j h) -> p h j", h=2))

        def open_group(s, i, half):
            n0 = half * HALF
            for h in range(2):
                nc.tensor.matmul_mx(
                    out=sums[s, i, half],
                    lhsT=codes2[s][:, h, 2 * i * P : 2 * (i + 1) * P].bitcast(E2M1),
                    lhsT_scale=plane2[:, h, s * SLICE + i * P : s * SLICE + (i + 1) * P],
                    rhs=u_codes[:, h * M + n0 : h * M + n0 + HALF].bitcast(E4M3),
                    rhs_scale=u_plane[:, h * M + n0 : h * M + n0 + HALF],
                    start=h == 0,
                    stop=False,
                )

        def close_group(s, i, half):
            n0 = half * HALF
            nc.tensor.matmul_mx(
                out=sums[s, i, half],
                lhsT=words1[s][:, i * P : (i + 1) * P].bitcast(E4M3),
                lhsT_scale=plane1[:, s * SLICE + i * P : s * SLICE + (i + 1) * P],
                rhs=w4_codes[:, 2 * n0 : 2 * (n0 + HALF)].bitcast(E2M1),
                rhs_scale=w4_plane[:, n0 : n0 + HALF],
                start=False,
                stop=True,
            )

        def open_slice(s):
            for i in range(tiles):
                bank = psum.tile([P, 2, HALF], F32, name=f"bank{s % 2 * 4 + i}")
                for half in range(2):
                    sums[s, i, half] = bank[:, half]
                if s == slices - 1:
                    other = psum.tile([P, 2, HALF], F32, name=f"bank{(s + 1) % 2 * 4 + i}")
                    sums[s, i, 1] = other[:, 1]
                sums[s, i] = bank
            for i in range(tiles):
                open_group(s, i, 0)
                if s == slices - 1:
                    open_group(s, i, 1)

        def close_slice(s):
            staged = keep.tile([P, tiles, M], F32, name=f"staged{s}")
            rows = out[s * SLICE : (s + 1) * SLICE, :].rearrange("(i p) n -> p i n", p=P)
            for i in range(tiles):
                if s < slices - 1:
                    close_group(s, i, 0)
                    open_group(s, i, 1)
                    close_group(s, i, 1)
                    nc.scalar.copy(staged[:, i], sums[s, i][:].rearrange("p h n -> p (h n)"))
                else:
                    for half in range(2):
                        close_group(s, i, half)
                    nc.scalar.copy(staged[:, i, 0:HALF], sums[s, i, 0])
                    nc.vector.tensor_copy(staged[:, i, HALF:M], sums[s, i, 1])
                    nc.sync.dma_start(rows[:, i], staged[:, i])
            if s < slices - 1:
                nc.sync.dma_start(rows, staged[:])

        gather_words(pairs, tab2_words, idx2, 0, "pairs")
        for s in range(slices):
            if s + 1 < slices:
                gather_words(pairs, tab2_words, idx2, s + 1, "pairs")
            part(s)
            open_slice(s)
            gather_words(words1, tab_words, idx1, s, "words1")
            close_slice(s)
